import numpy as np
import ml_dtypes


def mxq(x, axis, fmt="e4m3"):
    dtype, down = {"e4m3": (ml_dtypes.float8_e4m3fn, 7), "e5m2": (ml_dtypes.float8_e5m2, 14)}[fmt]
    v = np.moveaxis(np.asarray(x, np.float32).astype(ml_dtypes.bfloat16).astype(np.float64), axis, -1)
    blocks = v.reshape(v.shape[:-1] + (-1, 32))
    amax = np.abs(blocks).max(-1, keepdims=True)
    byte = np.maximum(np.where(amax > 0, np.frexp(amax)[1] - 1 + 127, 0) - down, 1)
    scale = np.exp2(byte - 127.0)
    codes = (blocks / scale).astype(np.float32).astype(dtype).astype(np.float64)
    return np.moveaxis((codes * scale).reshape(v.shape), -1, axis)


WIDE = False


def mx_kscale(k):
    if not WIDE:
        return np.ones(k)
    levels = np.array([10, -10, 5, -5, 0])
    if k % 512:
        return np.exp2(np.random.permutation(np.resize(levels, k // 32))).repeat(32)
    a = np.empty((k // 512, 16))
    for p in range(k // 512):
        a[p, :8] = np.random.permutation(np.resize(levels, 8))
        for g in range(8):
            far = levels[np.abs(levels - a[p, g]) >= 10]
            a[p, g + 8] = far[np.random.randint(len(far))]
    return np.exp2(a.ravel()).repeat(32)


def f64(x):
    return np.asarray(x).astype(np.float64)


def striped(idx):
    return np.tile(np.asarray(idx).reshape(-1, 16).T, (8, 1)).astype(np.uint16)


def unstriped(offs):
    return offs[:16].T.reshape(-1).astype(np.int64)


E2M1 = np.array([0.0, 0.5, 1.0, 1.5, 2.0, 3.0, 4.0, 6.0, -0.0, -0.5, -1.0, -1.5, -2.0, -3.0, -4.0, -6.0])


def pack_weight(w, fmt):
    k, n = w.shape
    w = f64(np.asarray(w, np.float32).astype(ml_dtypes.bfloat16)).reshape(k // 32, 32, n)
    amax = np.abs(w).max(1)
    if fmt == "e4m3":
        byte = np.frexp(amax)[1] - 1 + 127 - 7
    else:
        mant, ex = np.frexp(amax / 6.0)
        byte = np.where(mant > 0.5, ex, ex - 1) + 127
    byte = np.clip(np.where(amax > 0, byte, 1), 1, 254)
    scaled = (w * np.exp2(127.0 - byte)[:, None, :]).reshape(k, n).astype(np.float32)
    by_word = np.ascontiguousarray(scaled.reshape(k // 512, 128, 4, n).transpose(0, 1, 3, 2))
    if fmt == "e4m3":
        words = by_word.astype(ml_dtypes.float8_e4m3fn).view(np.uint8)
    else:
        c = by_word.astype(ml_dtypes.float4_e2m1fn).view(np.uint8) & 0xF
        words = (c[..., 0::2] | (c[..., 1::2] << 4)).reshape(k // 512, 128, 2 * n)
    return np.ascontiguousarray(words), np.ascontiguousarray(byte.astype(np.uint8).reshape(k // 512, 16, n))


def unpack_weight(words, scales, fmt):
    g, _, n = scales.shape
    words = np.ascontiguousarray(words).reshape(g, 128, n, -1)
    if fmt == "e4m3":
        vals = words.view(ml_dtypes.float8_e4m3fn).astype(np.float64)
    else:
        nib = np.empty((g, 128, n, 4), np.uint8)
        nib[..., 0::2] = words & 0xF
        nib[..., 1::2] = words >> 4
        vals = E2M1[nib]
    vals = vals * np.repeat(np.exp2(scales.astype(np.float64) - 127.0), 8, axis=1)[..., None]
    return vals.transpose(0, 1, 3, 2).reshape(g * 512, n)


def softplus(v):
    return np.log(1.0 + np.exp(v))


def sigmoid(v):
    return 1.0 / (1.0 + np.exp(-v))


D, E, T, I, Q = 512, 512, 2048, 512, 128


def setup_inputs():
    n = np.random.standard_normal
    idx = np.random.permutation(T)[:I]
    fd = mx_kscale(D)
    fe = mx_kscale(E)
    keysp = pack_weight(n((D, T)) / fd[:, None], "e2m1")
    valsp = pack_weight(n((E, T)) / fe[:, None], "e2m1")
    return {
        "query": (n((D, Q)) * 0.6 / np.sqrt(D) * fd[:, None]).astype(np.float32),
        "query2": (n((D, Q)) * 1.0 / np.sqrt(D) * fd[:, None]).astype(np.float32),
        "keys_words": keysp[0],
        "keys_scales": keysp[1],
        "strict": (np.random.uniform(0.4, 1.2, (Q, 1))).astype(np.float32),
        "gout": (n((E, Q)) * 1 / np.sqrt(E) * fe[:, None]).astype(np.float32),
        "vals_words": valsp[0],
        "vals_scales": valsp[1],
        "base": (0.5 * n((Q, I))).astype(np.float32),
        "offs": striped(idx),
    }


def reference(query, query2, keys_words, keys_scales, strict, gout, vals_words, vals_scales, base, offs):
    idx = unstriped(offs)
    keysu = unpack_weight(keys_words, keys_scales, "e2m1")
    valsu = unpack_weight(vals_words, vals_scales, "e2m1")
    queryq = mxq(f64(query), 0, "e4m3")
    keysidxg = keysu[:, idx]
    a = queryq.T @ keysidxg
    query2q = mxq(f64(query2), 0, "e4m3")
    b = query2q.T @ keysidxg
    s = a - softplus(b) * f64(strict)
    p = np.exp(s - np.max(s, axis=1, keepdims=True))
    z = np.sum(p, axis=1, keepdims=True)
    goutq = mxq(f64(gout), 0, "e4m3")
    valsidxg = valsu[:, idx]
    c0 = goutq.T @ valsidxg
    dz = np.sum(c0 * p / np.square(z) * (-1.0), axis=1, keepdims=True)
    dp = c0 / z + dz
    ds = dp * p
    db = ds * (-1.0) * f64(strict) * sigmoid(b)
    hdb = db * 512.0 * 2.0 * 512.0
    hds = hdb * sigmoid(b) * f64(strict) * (-1.0)
    hdp = hds * p
    hdz = np.sum(hdp, axis=1, keepdims=True)
    hz = np.sum(hdp * c0 / np.square(z) * (-1.0), axis=1, keepdims=True) + np.sum(hdz * (-1.0) * c0 * p / np.square(np.square(z)) * (-1.0), axis=1, keepdims=True) * z * 2.0
    hp = hds * dp + hdz * (-1.0) / np.square(z) * c0 + hz
    hs = hp * p
    hb = hdb * ds * (-1.0) * f64(strict) * sigmoid(b) * (1.0 - sigmoid(b)) + hs * (-1.0) * f64(strict) * sigmoid(b)
    y = hb + f64(base)
    return y

@@ -1,0 +1,156 @@
+from contextlib import ExitStack
+
+import concourse.mybir as mybir
+
+D, E, T, I, Q = 512, 512, 2048, 512, 128
+FLOPS = 3 * 2 * 512 * Q * I
+
+F32 = mybir.dt.float32
+BF16 = mybir.dt.bfloat16
+I32 = mybir.dt.int32
+U32 = mybir.dt.uint32
+U16 = mybir.dt.uint16
+U8 = mybir.dt.uint8
+FP8X4 = mybir.dt.float8_e4m3fn_x4
+FP4X4 = mybir.dt.float4_e2m1fn_x4
+ALU = mybir.AluOpType
+ACT = mybir.ActivationFunctionType
+AX = mybir.AxisListType
+
+P = 128
+PACK = 4
+HALF = I // 2
+CUBE_ROOT = float(512 * 2 * 512) ** (1.0 / 3.0)
+
+
+def tile_attend_gpheldback_kernel(tc, query, query2, keys_words, keys_scales, strict, gout,
+                                   vals_words, vals_scales, base, offs, out):
+    nc = tc.nc
+    halves = [slice(h * HALF, (h + 1) * HALF) for h in range(2)]
+
+    with ExitStack() as ctx:
+        sb = ctx.enter_context(tc.tile_pool(name="sb", bufs=1))
+        ps = ctx.enter_context(tc.psum_pool(name="ps", bufs=1))
+
+        def load_rows(name, src, tag):
+            raw = sb.tile([P, PACK, Q], F32, name=name, tag=tag, align_bytes=64)
+            nc.sync.dma_start(raw[:], src.rearrange("(p t) q -> p t q", t=PACK))
+            return raw
+
+        def round_rows(name, raw, copy, tag):
+            grouped = sb.tile([P, Q, PACK], BF16, name=name, tag=tag, align_bytes=64)
+            copy(grouped[:].rearrange("p (c i) t -> p c t i", i=4), raw[:].rearrange("p t (c i) -> p c t i", i=4))
+            return grouped
+
+        def quantise(name, grouped):
+            codes = sb.tile([P, Q], U32, name=name + "_codes", align_bytes=64)
+            scales = sb.tile([P, Q], U8, name=name + "_scales", align_bytes=64)
+            nc.vector.quantize_mx(out=codes[:].bitcast(FP8X4), scales=scales[:],
+                                  in_=grouped[:].rearrange("p q t -> p (q t)"))
+            return codes, scales
+
+        def load_scale_rows(tile, src, queue):
+            for g in range(4):
+                queue.dma_start(tile[32 * g:32 * g + 4, :].bitcast(I32), src[0, 4 * g:4 * g + 4, :].bitcast(I32))
+
+        def scores(acc, stationary, words, scale_bytes, cols):
+            codes, scales = stationary
+            nc.tensor.matmul_mx(out=acc, lhsT=codes[:].bitcast(FP8X4), lhsT_scale=scales[:],
+                                rhs=words[:, cols].bitcast(FP4X4), rhs_scale=scale_bytes[:, cols],
+                                start=True, stop=True)
+
+        def column(name):
+            return sb.tile([P, 1], F32, name=name)
+
+        def wide(name):
+            return sb.tile([P, I], F32, name=name)
+
+        offsets = sb.tile([P, I // 16], U16, name="offsets")
+        nc.sync.dma_start(offsets[:], offs)
+
+        key_scale_pool = sb.tile([P, T], U8, name="key_scale_pool")
+        nc.gpsimd.memset(key_scale_pool[:].bitcast(I32), 0)
+        load_scale_rows(key_scale_pool, keys_scales, nc.scalar)
+        val_scale_pool = sb.tile([P, T], U8, name="val_scale_pool")
+        nc.vector.memset(val_scale_pool[:].bitcast(I32), 0)
+
+        query2_raw = load_rows("query2_raw", query2, "slot_a")
+        key_word_pool = sb.tile([P, T], U16, name="key_word_pool", tag="slot_c")
+        nc.sync.dma_start(key_word_pool[:].bitcast(I32), keys_words[0].bitcast(I32))
+        query_raw = load_rows("query_raw", query, "slot_b")
+        r = column("r")
+        nc.gpsimd.dma_start(r[:], strict)
+        load_scale_rows(val_scale_pool, vals_scales, nc.sync)
+
+        query2_bf = round_rows("query2_bf", query2_raw, nc.scalar.copy, "slot_d")
+        val_word_pool = sb.tile([P, T], U16, name="val_word_pool", tag="slot_a", align_bytes=64)
+        nc.sync.dma_start(val_word_pool[:].bitcast(I32), vals_words[0].bitcast(I32))
+        query_bf = round_rows("query_bf", query_raw, nc.scalar.copy, "query_bf")
+        one_plus_r = column("one_plus_r")
+        nc.scalar.activation(one_plus_r[:], r[:], ACT.Identity, bias=1.0)
+
+        key_scales = sb.tile([P, I], U8, name="key_scales", align_bytes=64)
+        nc.vector.tensor_copy(key_scales[:], key_scale_pool[:].indirect(offsets[:]))
+        query2_mx = quantise("query2", query2_bf)
+        gout_raw = load_rows("gout_raw", gout, "slot_d")
+        key_words = sb.tile([P, I], U16, name="key_words", align_bytes=64)
+        b = ps.tile([P, I], F32, name="b")
+        tanh_b, abs_tanh, neg_log = wide("tanh_b"), wide("abs_tanh"), wide("neg_log")
+        for h, cols in enumerate(halves):
+            nc.vector.tensor_copy(key_words[:, cols],
+                                  key_word_pool[:].indirect(offsets[:, h * HALF // 16:(h + 1) * HALF // 16]))
+            scores(b[:, cols], query2_mx, key_words, key_scales, cols)
+            nc.scalar.activation(tanh_b[:, cols], b[:, cols], ACT.Tanh, scale=0.5)
+            nc.scalar.activation(abs_tanh[:, cols], tanh_b[:, cols], ACT.Abs)
+        base_sb = sb.tile([P, I], F32, name="base_sb", tag="slot_c")
+        nc.sync.dma_start(base_sb[:], base)
+        for cols in halves:
+            nc.scalar.activation(neg_log[:, cols], abs_tanh[:, cols], ACT.Ln, scale=0.5, bias=0.5)
+
+        query_mx = quantise("query", query_bf)
+        a = ps.tile([P, I], F32, name="a")
+        scores(a[:], query_mx, key_words, key_scales, slice(0, I))
+
+        val_scales = sb.tile([P, I], U8, name="val_scales", align_bytes=64)
+        nc.vector.tensor_copy(val_scales[:], val_scale_pool[:].indirect(offsets[:]))
+        val_words = sb.tile([P, I], U16, name="val_words", align_bytes=64)
+        nc.vector.tensor_copy(val_words[:], val_word_pool[:].indirect(offsets[:]))
+        gout_bf = round_rows("gout_bf", gout_raw, nc.vector.tensor_copy, "slot_a")
+        gout_mx = quantise("gout", gout_bf)
+        c0 = ps.tile([P, I], F32, name="c0")
+        scores(c0[:], gout_mx, val_words, val_scales, slice(0, I))
+
+        softplus = sb.tile([P, I], F32, name="softplus", tag="slot_d", align_bytes=64)
+        neg_s, log_sig = wide("neg_s"), wide("log_sig")
+        for cols in halves:
+            nc.vector.scalar_tensor_tensor(softplus[:, cols], b[:, cols], 0.0, neg_log[:, cols], ALU.max, ALU.subtract)
+        for cols in halves:
+            nc.vector.scalar_tensor_tensor(neg_s[:, cols], softplus[:, cols], r[:], a[:, cols], ALU.mult, ALU.subtract)
+        neg_max = column("neg_max")
+        nc.vector.tensor_reduce(neg_max[:], neg_s[:], AX.X, ALU.min)
+        p, z = wide("p"), column("z")
+        nc.scalar.activation(p[:], neg_s[:], ACT.Exp, scale=-1.0, bias=neg_max[:], accum_out=z[:])
+        nc.vector.scalar_tensor_tensor(log_sig[:], b[:], 0.0, neg_log[:], ALU.min, ALU.add)
+        sig, neg_f = wide("sig"), wide("neg_f")
+        nc.scalar.activation(sig[:], log_sig[:], ACT.Exp)
+        nc.scalar.activation(neg_f[:], sig[:], ACT.Identity, scale=one_plus_r[:], bias=-1.0)
+
+        rz, rho, c_mean, w_c = column("rz"), column("rho"), column("c_mean"), wide("w_c")
+        nc.vector.reciprocal(rz[:], z[:])
+        nc.vector.scalar_tensor_tensor(w_c[:], c0[:], rz[:], p[:], ALU.mult, ALU.mult, accum_out=c_mean[:])
+        nc.vector.tensor_scalar(rho[:], rz[:], r[:], CUBE_ROOT, ALU.mult, ALU.mult)
+        g, gu = wide("g"), wide("gu")
+        nc.vector.scalar_tensor_tensor(g[:], sig[:], rho[:], p[:], ALU.mult, ALU.mult)
+        nc.vector.scalar_tensor_tensor(gu[:], c0[:], c_mean[:], g[:], ALU.subtract, ALU.mult)
+        ggu, a_sum = wide("ggu"), column("a_sum")
+        nc.vector.scalar_tensor_tensor(ggu[:], gu[:], 1.0, g[:], ALU.mult, ALU.mult, accum_out=a_sum[:])
+        gu2, b_sum = wide("gu2"), column("b_sum")
+        nc.scalar.activation(gu2[:], gu[:], ACT.Square, accum_out=b_sum[:])
+        x, part1, part2, res = wide("x"), wide("part1"), wide("part2"), wide("res")
+        nc.vector.scalar_tensor_tensor(x[:], gu2[:], -CUBE_ROOT, neg_f[:], ALU.mult, ALU.mult)
+        nc.vector.scalar_tensor_tensor(part1[:], gu[:], a_sum[:], base_sb[:], ALU.mult, ALU.add)
+        for cols in halves:
+            nc.vector.scalar_tensor_tensor(part2[:, cols], g[:, cols], b_sum[:], x[:, cols], ALU.mult, ALU.add)
+        for cols, queue in zip(halves, (nc.sync, nc.scalar)):
+            nc.vector.tensor_tensor(res[:, cols], part1[:, cols], part2[:, cols], ALU.add)
+            queue.dma_start(out[:, cols], res[:, cols])

@@ -32,8 +32,8 @@ def tile_attend_gpheldback_kernel(tc, query, query2, keys_words, keys_scales, st
         sb = ctx.enter_context(tc.tile_pool(name="sb", bufs=1))
         ps = ctx.enter_context(tc.psum_pool(name="ps", bufs=1))
 
-        def load_rows(name, src, tag):
-            raw = sb.tile([P, PACK, Q], F32, name=name, tag=tag, align_bytes=64)
+        def load_rows(name, src):
+            raw = sb.tile([P, PACK, Q], F32, name=name)
             nc.sync.dma_start(raw[:], src.rearrange("(p t) q -> p t q", t=PACK))
             return raw
 
@@ -49,9 +49,12 @@ def tile_attend_gpheldback_kernel(tc, query, query2, keys_words, keys_scales, st
                                   in_=grouped[:].rearrange("p q t -> p (q t)"))
             return codes, scales
 
-        def load_scale_rows(tile, src, queue):
+        def load_scale_rows(name, src, tag):
+            tile = sb.tile([P, T], U8, name=name, tag=tag, align_bytes=64)
             for g in range(4):
-                queue.dma_start(tile[32 * g:32 * g + 4, :].bitcast(I32), src[0, 4 * g:4 * g + 4, :].bitcast(I32))
+                rows = src[0:1, 4 * g:4 * g + 4, :].bitcast(I32)
+                nc.sync.dma_start(tile[32 * g:32 * g + 32, :].bitcast(I32), rows.to_broadcast([8, 4, T // 4]))
+            return tile
 
         def scores(acc, stationary, words, scale_bytes, cols):
             codes, scales = stationary
@@ -68,32 +71,31 @@ def tile_attend_gpheldback_kernel(tc, query, query2, keys_words, keys_scales, st
         offsets = sb.tile([P, I // 16], U16, name="offsets")
         nc.sync.dma_start(offsets[:], offs)
 
-        key_scale_pool = sb.tile([P, T], U8, name="key_scale_pool")
-        nc.gpsimd.memset(key_scale_pool[:].bitcast(I32), 0)
-        load_scale_rows(key_scale_pool, keys_scales, nc.scalar)
-        val_scale_pool = sb.tile([P, T], U8, name="val_scale_pool")
-        nc.vector.memset(val_scale_pool[:].bitcast(I32), 0)
-
-        query2_raw = load_rows("query2_raw", query2, "slot_a")
-        key_word_pool = sb.tile([P, T], U16, name="key_word_pool", tag="slot_c")
+        key_scale_pool = load_scale_rows("key_scale_pool", keys_scales, "key_scale_pool")
+        query2_raw = load_rows("query2_raw", query2)
+        key_word_pool = sb.tile([P, T], U16, name="key_word_pool")
         nc.sync.dma_start(key_word_pool[:].bitcast(I32), keys_words[0].bitcast(I32))
-        query_raw = load_rows("query_raw", query, "slot_b")
+        query_raw = load_rows("query_raw", query)
+        val_word_pool = sb.tile([P, T], U16, name="val_word_pool")
+        nc.sync.dma_start(val_word_pool[:].bitcast(I32), vals_words[0].bitcast(I32))
+        gout_raw = load_rows("gout_raw", gout)
+        val_scale_pool = load_scale_rows("val_scale_pool", vals_scales, "slot_e")
+        base_sb = wide("base_sb")
+        nc.sync.dma_start(base_sb[:], base)
         r = column("r")
         nc.gpsimd.dma_start(r[:], strict)
-        load_scale_rows(val_scale_pool, vals_scales, nc.sync)
 
         query2_bf = round_rows("query2_bf", query2_raw, nc.scalar.copy, "slot_d")
-        val_word_pool = sb.tile([P, T], U16, name="val_word_pool", tag="slot_a", align_bytes=64)
-        nc.sync.dma_start(val_word_pool[:].bitcast(I32), vals_words[0].bitcast(I32))
         query_bf = round_rows("query_bf", query_raw, nc.scalar.copy, "query_bf")
-        one_plus_r = column("one_plus_r")
-        nc.scalar.activation(one_plus_r[:], r[:], ACT.Identity, bias=1.0)
+        r_c, f_slope, f_offset = column("r_c"), column("f_slope"), column("f_offset")
+        nc.gpsimd.tensor_scalar(r_c[:], r[:], CUBE_ROOT, 0.0, ALU.mult, ALU.add)
+        nc.gpsimd.tensor_scalar(f_slope[:], r[:], -CUBE_ROOT, -CUBE_ROOT, ALU.mult, ALU.add)
+        nc.gpsimd.tensor_scalar(f_offset[:], r[:], 0.0, CUBE_ROOT, ALU.mult, ALU.add)
 
         key_scales = sb.tile([P, I], U8, name="key_scales", align_bytes=64)
         nc.vector.tensor_copy(key_scales[:], key_scale_pool[:].indirect(offsets[:]))
         query2_mx = quantise("query2", query2_bf)
-        gout_raw = load_rows("gout_raw", gout, "slot_d")
-        key_words = sb.tile([P, I], U16, name="key_words", align_bytes=64)
+        key_words = sb.tile([P, I], U16, name="key_words", tag="slot_d", align_bytes=64)
         b = ps.tile([P, I], F32, name="b")
         tanh_b, abs_tanh, neg_log = wide("tanh_b"), wide("abs_tanh"), wide("neg_log")
         for h, cols in enumerate(halves):
@@ -102,8 +104,6 @@ def tile_attend_gpheldback_kernel(tc, query, query2, keys_words, keys_scales, st
             scores(b[:, cols], query2_mx, key_words, key_scales, cols)
             nc.scalar.activation(tanh_b[:, cols], b[:, cols], ACT.Tanh, scale=0.5)
             nc.scalar.activation(abs_tanh[:, cols], tanh_b[:, cols], ACT.Abs)
-        base_sb = sb.tile([P, I], F32, name="base_sb", tag="slot_c")
-        nc.sync.dma_start(base_sb[:], base)
         for cols in halves:
             nc.scalar.activation(neg_log[:, cols], abs_tanh[:, cols], ACT.Ln, scale=0.5, bias=0.5)
 
@@ -111,16 +111,16 @@ def tile_attend_gpheldback_kernel(tc, query, query2, keys_words, keys_scales, st
         a = ps.tile([P, I], F32, name="a")
         scores(a[:], query_mx, key_words, key_scales, slice(0, I))
 
-        val_scales = sb.tile([P, I], U8, name="val_scales", align_bytes=64)
-        nc.vector.tensor_copy(val_scales[:], val_scale_pool[:].indirect(offsets[:]))
         val_words = sb.tile([P, I], U16, name="val_words", align_bytes=64)
         nc.vector.tensor_copy(val_words[:], val_word_pool[:].indirect(offsets[:]))
-        gout_bf = round_rows("gout_bf", gout_raw, nc.vector.tensor_copy, "slot_a")
+        gout_bf = round_rows("gout_bf", gout_raw, nc.vector.tensor_copy, "gout_bf")
+        val_scales = sb.tile([P, I], U8, name="val_scales", align_bytes=64)
+        nc.vector.tensor_copy(val_scales[:], val_scale_pool[:].indirect(offsets[:]))
         gout_mx = quantise("gout", gout_bf)
         c0 = ps.tile([P, I], F32, name="c0")
         scores(c0[:], gout_mx, val_words, val_scales, slice(0, I))
 
-        softplus = sb.tile([P, I], F32, name="softplus", tag="slot_d", align_bytes=64)
+        softplus = sb.tile([P, I], F32, name="softplus", tag="slot_e", align_bytes=64)
         neg_s, log_sig = wide("neg_s"), wide("log_sig")
         for cols in halves:
             nc.vector.scalar_tensor_tensor(softplus[:, cols], b[:, cols], 0.0, neg_log[:, cols], ALU.max, ALU.subtract)
@@ -131,26 +131,38 @@ def tile_attend_gpheldback_kernel(tc, query, query2, keys_words, keys_scales, st
         p, z = wide("p"), column("z")
         nc.scalar.activation(p[:], neg_s[:], ACT.Exp, scale=-1.0, bias=neg_max[:], accum_out=z[:])
         nc.vector.scalar_tensor_tensor(log_sig[:], b[:], 0.0, neg_log[:], ALU.min, ALU.add)
-        sig, neg_f = wide("sig"), wide("neg_f")
+        sig, f = wide("sig"), wide("f")
         nc.scalar.activation(sig[:], log_sig[:], ACT.Exp)
-        nc.scalar.activation(neg_f[:], sig[:], ACT.Identity, scale=one_plus_r[:], bias=-1.0)
+        nc.scalar.activation(f[:], sig[:], ACT.Identity, scale=f_slope[:], bias=f_offset[:])
 
-        rz, rho, c_mean, w_c = column("rz"), column("rho"), column("c_mean"), wide("w_c")
+        rz, pc_sum, c_mean, pc = column("rz"), column("pc_sum"), column("c_mean"), wide("pc")
+        g, gu, w = wide("g"), wide("gu"), wide("w")
+        nc.vector.scalar_tensor_tensor(pc[:], c0[:], 1.0, p[:], ALU.mult, ALU.mult, accum_out=pc_sum[:])
         nc.vector.reciprocal(rz[:], z[:])
-        nc.vector.scalar_tensor_tensor(w_c[:], c0[:], rz[:], p[:], ALU.mult, ALU.mult, accum_out=c_mean[:])
-        nc.vector.tensor_scalar(rho[:], rz[:], r[:], CUBE_ROOT, ALU.mult, ALU.mult)
-        g, gu = wide("g"), wide("gu")
-        nc.vector.scalar_tensor_tensor(g[:], sig[:], rho[:], p[:], ALU.mult, ALU.mult)
-        nc.vector.scalar_tensor_tensor(gu[:], c0[:], c_mean[:], g[:], ALU.subtract, ALU.mult)
-        ggu, a_sum = wide("ggu"), column("a_sum")
-        nc.vector.scalar_tensor_tensor(ggu[:], gu[:], 1.0, g[:], ALU.mult, ALU.mult, accum_out=a_sum[:])
-        gu2, b_sum = wide("gu2"), column("b_sum")
-        nc.scalar.activation(gu2[:], gu[:], ACT.Square, accum_out=b_sum[:])
-        x, part1, part2, res = wide("x"), wide("part1"), wide("part2"), wide("res")
-        nc.vector.scalar_tensor_tensor(x[:], gu2[:], -CUBE_ROOT, neg_f[:], ALU.mult, ALU.mult)
-        nc.vector.scalar_tensor_tensor(part1[:], gu[:], a_sum[:], base_sb[:], ALU.mult, ALU.add)
+        nc.vector.tensor_tensor(g[:, halves[0]], sig[:, halves[0]], p[:, halves[0]], ALU.mult)
+        nc.vector.tensor_scalar(c_mean[:], pc_sum[:], rz[:], None, ALU.mult)
+        nc.vector.tensor_tensor(g[:, halves[1]], sig[:, halves[1]], p[:, halves[1]], ALU.mult)
+        rho, rho2, rho3 = column("rho"), column("rho2"), column("rho3")
+        nc.scalar.activation(rho[:], rz[:], ACT.Copy, scale=r_c[:])
+        nc.scalar.activation(rho2[:], rz[:], ACT.Square, scale=r_c[:])
+        nc.scalar.activation(rho3[:], rho2[:], ACT.Copy, scale=rho[:])
         for cols in halves:
-            nc.vector.scalar_tensor_tensor(part2[:, cols], g[:, cols], b_sum[:], x[:, cols], ALU.mult, ALU.add)
+            nc.vector.scalar_tensor_tensor(gu[:, cols], c0[:, cols], c_mean[:], g[:, cols], ALU.subtract, ALU.mult)
+        gu2, gu2_sum, b_sum = wide("gu2"), column("gu2_sum"), column("b_sum")
+        nc.scalar.activation(gu2[:], gu[:], ACT.Square, scale=rho[:], accum_out=gu2_sum[:])
+        nc.scalar.activation(b_sum[:], gu2_sum[:], ACT.Copy, scale=rho[:])
+        ggu, a_sum = wide("ggu"), column("a_sum")
+
+        def guf(cols):
+            nc.vector.scalar_tensor_tensor(w[:, cols], gu[:, cols], rho2[:], f[:, cols], ALU.mult, ALU.mult)
+
+        guf(halves[0])
+        nc.vector.scalar_tensor_tensor(ggu[:], gu[:], rho3[:], g[:], ALU.mult, ALU.mult, accum_out=a_sum[:])
+        guf(halves[1])
+        part1, part2, res = wide("part1"), wide("part2"), wide("res")
+        nc.vector.scalar_tensor_tensor(part1[:], g[:], b_sum[:], base_sb[:], ALU.mult, ALU.add)
+        for cols in halves:
+            nc.vector.scalar_tensor_tensor(part2[:, cols], w[:, cols], a_sum[:], gu[:, cols], ALU.add, ALU.mult)
         for cols, queue in zip(halves, (nc.sync, nc.scalar)):
             nc.vector.tensor_tensor(res[:, cols], part1[:, cols], part2[:, cols], ALU.add)
             queue.dma_start(out[:, cols], res[:, cols])

@@ -20,6 +20,7 @@ AX = mybir.AxisListType
 P = 128
 PACK = 4
 HALF = I // 2
+LAST = 128
 CUBE_ROOT = float(512 * 2 * 512) ** (1.0 / 3.0)
 
 
@@ -32,8 +33,8 @@ def tile_attend_gpheldback_kernel(tc, query, query2, keys_words, keys_scales, st
         sb = ctx.enter_context(tc.tile_pool(name="sb", bufs=1))
         ps = ctx.enter_context(tc.psum_pool(name="ps", bufs=1))
 
-        def load_rows(name, src):
-            raw = sb.tile([P, PACK, Q], F32, name=name)
+        def load_rows(name, src, tag):
+            raw = sb.tile([P, PACK, Q], F32, name=name, tag=tag, align_bytes=64)
             nc.sync.dma_start(raw[:], src.rearrange("(p t) q -> p t q", t=PACK))
             return raw
 
@@ -42,8 +43,8 @@ def tile_attend_gpheldback_kernel(tc, query, query2, keys_words, keys_scales, st
             copy(grouped[:].rearrange("p (c i) t -> p c t i", i=4), raw[:].rearrange("p t (c i) -> p c t i", i=4))
             return grouped
 
-        def quantise(name, grouped):
-            codes = sb.tile([P, Q], U32, name=name + "_codes", align_bytes=64)
+        def quantise(name, grouped, tag):
+            codes = sb.tile([P, Q], U32, name=name + "_codes", tag=tag, align_bytes=64)
             scales = sb.tile([P, Q], U8, name=name + "_scales", align_bytes=64)
             nc.vector.quantize_mx(out=codes[:].bitcast(FP8X4), scales=scales[:],
                                   in_=grouped[:].rearrange("p q t -> p (q t)"))
@@ -51,9 +52,9 @@ def tile_attend_gpheldback_kernel(tc, query, query2, keys_words, keys_scales, st
 
         def load_scale_rows(name, src, tag):
             tile = sb.tile([P, T], U8, name=name, tag=tag, align_bytes=64)
+            nc.vector.memset(tile[:].bitcast(I32), 0)
             for g in range(4):
-                rows = src[0:1, 4 * g:4 * g + 4, :].bitcast(I32)
-                nc.sync.dma_start(tile[32 * g:32 * g + 32, :].bitcast(I32), rows.to_broadcast([8, 4, T // 4]))
+                nc.sync.dma_start(tile[32 * g:32 * g + 4, :].bitcast(I32), src[0, 4 * g:4 * g + 4, :].bitcast(I32))
             return tile
 
         def scores(acc, stationary, words, scale_bytes, cols):
@@ -71,56 +72,56 @@ def tile_attend_gpheldback_kernel(tc, query, query2, keys_words, keys_scales, st
         offsets = sb.tile([P, I // 16], U16, name="offsets")
         nc.sync.dma_start(offsets[:], offs)
 
-        key_scale_pool = load_scale_rows("key_scale_pool", keys_scales, "key_scale_pool")
-        query2_raw = load_rows("query2_raw", query2)
         key_word_pool = sb.tile([P, T], U16, name="key_word_pool")
         nc.sync.dma_start(key_word_pool[:].bitcast(I32), keys_words[0].bitcast(I32))
-        query_raw = load_rows("query_raw", query)
-        val_word_pool = sb.tile([P, T], U16, name="val_word_pool")
-        nc.sync.dma_start(val_word_pool[:].bitcast(I32), vals_words[0].bitcast(I32))
-        gout_raw = load_rows("gout_raw", gout)
+        query2_raw = load_rows("query2_raw", query2, "slot_a")
+        query_raw = load_rows("query_raw", query, "slot_b")
+        key_scale_pool = load_scale_rows("key_scale_pool", keys_scales, "slot_c")
         val_scale_pool = load_scale_rows("val_scale_pool", vals_scales, "slot_e")
-        base_sb = wide("base_sb")
-        nc.sync.dma_start(base_sb[:], base)
         r = column("r")
         nc.gpsimd.dma_start(r[:], strict)
 
         query2_bf = round_rows("query2_bf", query2_raw, nc.scalar.copy, "slot_d")
+        val_word_pool = sb.tile([P, T], U16, name="val_word_pool", tag="slot_a", align_bytes=64)
+        nc.sync.dma_start(val_word_pool[:].bitcast(I32), vals_words[0].bitcast(I32))
         query_bf = round_rows("query_bf", query_raw, nc.scalar.copy, "query_bf")
+        gout_raw = load_rows("gout_raw", gout, "slot_b")
         r_c, f_slope, f_offset = column("r_c"), column("f_slope"), column("f_offset")
         nc.gpsimd.tensor_scalar(r_c[:], r[:], CUBE_ROOT, 0.0, ALU.mult, ALU.add)
         nc.gpsimd.tensor_scalar(f_slope[:], r[:], -CUBE_ROOT, -CUBE_ROOT, ALU.mult, ALU.add)
         nc.gpsimd.tensor_scalar(f_offset[:], r[:], 0.0, CUBE_ROOT, ALU.mult, ALU.add)
 
-        key_scales = sb.tile([P, I], U8, name="key_scales", align_bytes=64)
-        nc.vector.tensor_copy(key_scales[:], key_scale_pool[:].indirect(offsets[:]))
-        query2_mx = quantise("query2", query2_bf)
-        key_words = sb.tile([P, I], U16, name="key_words", tag="slot_d", align_bytes=64)
+        key_words = sb.tile([P, I], U16, name="key_words", align_bytes=64)
+        nc.vector.tensor_copy(key_words[:], key_word_pool[:].indirect(offsets[:]))
+        query2_mx = quantise("query2", query2_bf, "query2_codes")
+        key_scales = sb.tile([P, I], U8, name="key_scales", tag="slot_d", align_bytes=64)
         b = ps.tile([P, I], F32, name="b")
         tanh_b, abs_tanh, neg_log = wide("tanh_b"), wide("abs_tanh"), wide("neg_log")
         for h, cols in enumerate(halves):
-            nc.vector.tensor_copy(key_words[:, cols],
-                                  key_word_pool[:].indirect(offsets[:, h * HALF // 16:(h + 1) * HALF // 16]))
+            nc.vector.tensor_copy(key_scales[:, cols],
+                                  key_scale_pool[:].indirect(offsets[:, h * HALF // 16:(h + 1) * HALF // 16]))
             scores(b[:, cols], query2_mx, key_words, key_scales, cols)
             nc.scalar.activation(tanh_b[:, cols], b[:, cols], ACT.Tanh, scale=0.5)
             nc.scalar.activation(abs_tanh[:, cols], tanh_b[:, cols], ACT.Abs)
         for cols in halves:
             nc.scalar.activation(neg_log[:, cols], abs_tanh[:, cols], ACT.Ln, scale=0.5, bias=0.5)
 
-        query_mx = quantise("query", query_bf)
+        query_mx = quantise("query", query_bf, "slot_c")
         a = ps.tile([P, I], F32, name="a")
         scores(a[:], query_mx, key_words, key_scales, slice(0, I))
 
-        val_words = sb.tile([P, I], U16, name="val_words", align_bytes=64)
-        nc.vector.tensor_copy(val_words[:], val_word_pool[:].indirect(offsets[:]))
-        gout_bf = round_rows("gout_bf", gout_raw, nc.vector.tensor_copy, "gout_bf")
+        base_sb = sb.tile([P, I], F32, name="base_sb", tag="slot_c", align_bytes=64)
+        nc.sync.dma_start(base_sb[:], base)
         val_scales = sb.tile([P, I], U8, name="val_scales", align_bytes=64)
         nc.vector.tensor_copy(val_scales[:], val_scale_pool[:].indirect(offsets[:]))
-        gout_mx = quantise("gout", gout_bf)
+        val_words = sb.tile([P, I], U16, name="val_words", tag="slot_e", align_bytes=64)
+        nc.vector.tensor_copy(val_words[:], val_word_pool[:].indirect(offsets[:]))
+        gout_bf = round_rows("gout_bf", gout_raw, nc.vector.tensor_copy, "slot_a")
+        gout_mx = quantise("gout", gout_bf, "gout_codes")
         c0 = ps.tile([P, I], F32, name="c0")
         scores(c0[:], gout_mx, val_words, val_scales, slice(0, I))
 
-        softplus = sb.tile([P, I], F32, name="softplus", tag="slot_e", align_bytes=64)
+        softplus = sb.tile([P, I], F32, name="softplus", tag="slot_b", align_bytes=64)
         neg_s, log_sig = wide("neg_s"), wide("log_sig")
         for cols in halves:
             nc.vector.scalar_tensor_tensor(softplus[:, cols], b[:, cols], 0.0, neg_log[:, cols], ALU.max, ALU.subtract)
@@ -161,8 +162,9 @@ def tile_attend_gpheldback_kernel(tc, query, query2, keys_words, keys_scales, st
         guf(halves[1])
         part1, part2, res = wide("part1"), wide("part2"), wide("res")
         nc.vector.scalar_tensor_tensor(part1[:], g[:], b_sum[:], base_sb[:], ALU.mult, ALU.add)
-        for cols in halves:
+        pieces = (slice(0, I - LAST), slice(I - LAST, I))
+        for cols in pieces:
             nc.vector.scalar_tensor_tensor(part2[:, cols], w[:, cols], a_sum[:], gu[:, cols], ALU.add, ALU.mult)
-        for cols, queue in zip(halves, (nc.sync, nc.scalar)):
+        for cols, queue in zip(pieces, (nc.scalar, nc.sync)):
             nc.vector.tensor_tensor(res[:, cols], part1[:, cols], part2[:, cols], ALU.add)
             queue.dma_start(out[:, cols], res[:, cols])

@@ -95,13 +95,13 @@ def tile_attend_gpheldback_kernel(tc, query, query2, keys_words, keys_scales, st
         nc.vector.tensor_copy(key_words[:], key_word_pool[:].indirect(offsets[:]))
         query2_mx = quantise("query2", query2_bf, "query2_codes")
         key_scales = sb.tile([P, I], U8, name="key_scales", tag="slot_d", align_bytes=64)
-        b = ps.tile([P, I], F32, name="b")
+        b = [ps.tile([P, HALF], F32, name="b%d" % h) for h in range(2)]
         tanh_b, abs_tanh, neg_log = wide("tanh_b"), wide("abs_tanh"), wide("neg_log")
         for h, cols in enumerate(halves):
             nc.vector.tensor_copy(key_scales[:, cols],
                                   key_scale_pool[:].indirect(offsets[:, h * HALF // 16:(h + 1) * HALF // 16]))
-            scores(b[:, cols], query2_mx, key_words, key_scales, cols)
-            nc.scalar.activation(tanh_b[:, cols], b[:, cols], ACT.Tanh, scale=0.5)
+            scores(b[h][:], query2_mx, key_words, key_scales, cols)
+            nc.scalar.activation(tanh_b[:, cols], b[h][:], ACT.Tanh, scale=0.5)
             nc.scalar.activation(abs_tanh[:, cols], tanh_b[:, cols], ACT.Abs)
         for cols in halves:
             nc.scalar.activation(neg_log[:, cols], abs_tanh[:, cols], ACT.Ln, scale=0.5, bias=0.5)
@@ -123,15 +123,16 @@ def tile_attend_gpheldback_kernel(tc, query, query2, keys_words, keys_scales, st
 
         softplus = sb.tile([P, I], F32, name="softplus", tag="slot_b", align_bytes=64)
         neg_s, log_sig = wide("neg_s"), wide("log_sig")
-        for cols in halves:
-            nc.vector.scalar_tensor_tensor(softplus[:, cols], b[:, cols], 0.0, neg_log[:, cols], ALU.max, ALU.subtract)
+        for h, cols in enumerate(halves):
+            nc.vector.scalar_tensor_tensor(softplus[:, cols], b[h][:], 0.0, neg_log[:, cols], ALU.max, ALU.subtract)
         for cols in halves:
             nc.vector.scalar_tensor_tensor(neg_s[:, cols], softplus[:, cols], r[:], a[:, cols], ALU.mult, ALU.subtract)
         neg_max = column("neg_max")
         nc.vector.tensor_reduce(neg_max[:], neg_s[:], AX.X, ALU.min)
         p, z = wide("p"), column("z")
         nc.scalar.activation(p[:], neg_s[:], ACT.Exp, scale=-1.0, bias=neg_max[:], accum_out=z[:])
-        nc.vector.scalar_tensor_tensor(log_sig[:], b[:], 0.0, neg_log[:], ALU.min, ALU.add)
+        for h, cols in enumerate(halves):
+            nc.vector.scalar_tensor_tensor(log_sig[:, cols], b[h][:], 0.0, neg_log[:, cols], ALU.min, ALU.add)
         sig, f = wide("sig"), wide("f")
         nc.scalar.activation(sig[:], log_sig[:], ACT.Exp)
         nc.scalar.activation(f[:], sig[:], ACT.Identity, scale=f_slope[:], bias=f_offset[:])

from contextlib import ExitStack

import concourse.mybir as mybir

D, E, T, I, Q = 512, 512, 2048, 512, 128
FLOPS = 3 * 2 * 512 * Q * I

F32 = mybir.dt.float32
BF16 = mybir.dt.bfloat16
I32 = mybir.dt.int32
U32 = mybir.dt.uint32
U16 = mybir.dt.uint16
U8 = mybir.dt.uint8
FP8X4 = mybir.dt.float8_e4m3fn_x4
FP4X4 = mybir.dt.float4_e2m1fn_x4
ALU = mybir.AluOpType
ACT = mybir.ActivationFunctionType
AX = mybir.AxisListType

P = 128
PACK = 4
HALF = I // 2
LAST = 128
CUBE_ROOT = float(512 * 2 * 512) ** (1.0 / 3.0)


def tile_attend_gpheldback_kernel(tc, query, query2, keys_words, keys_scales, strict, gout,
                                   vals_words, vals_scales, base, offs, out):
    nc = tc.nc
    halves = [slice(h * HALF, (h + 1) * HALF) for h in range(2)]

    with ExitStack() as ctx:
        sb = ctx.enter_context(tc.tile_pool(name="sb", bufs=1))
        ps = ctx.enter_context(tc.psum_pool(name="ps", bufs=1))

        def load_rows(name, src, tag):
            raw = sb.tile([P, PACK, Q], F32, name=name, tag=tag, align_bytes=64)
            nc.sync.dma_start(raw[:], src.rearrange("(p t) q -> p t q", t=PACK))
            return raw

        def round_rows(name, raw, copy, tag):
            grouped = sb.tile([P, Q, PACK], BF16, name=name, tag=tag, align_bytes=64)
            copy(grouped[:].rearrange("p (c i) t -> p c t i", i=4), raw[:].rearrange("p t (c i) -> p c t i", i=4))
            return grouped

        def quantise(name, grouped, tag):
            codes = sb.tile([P, Q], U32, name=name + "_codes", tag=tag, align_bytes=64)
            scales = sb.tile([P, Q], U8, name=name + "_scales", align_bytes=64)
            nc.vector.quantize_mx(out=codes[:].bitcast(FP8X4), scales=scales[:],
                                  in_=grouped[:].rearrange("p q t -> p (q t)"))
            return codes, scales

        def load_scale_rows(name, src, tag):
            tile = sb.tile([P, T], U8, name=name, tag=tag, align_bytes=64)
            nc.vector.memset(tile[:].bitcast(I32), 0)
            for g in range(4):
                nc.sync.dma_start(tile[32 * g:32 * g + 4, :].bitcast(I32), src[0, 4 * g:4 * g + 4, :].bitcast(I32))
            return tile

        def scores(acc, stationary, words, scale_bytes, cols):
            codes, scales = stationary
            nc.tensor.matmul_mx(out=acc, lhsT=codes[:].bitcast(FP8X4), lhsT_scale=scales[:],
                                rhs=words[:, cols].bitcast(FP4X4), rhs_scale=scale_bytes[:, cols],
                                start=True, stop=True)

        def column(name):
            return sb.tile([P, 1], F32, name=name)

        def wide(name):
            return sb.tile([P, I], F32, name=name)

        offsets = sb.tile([P, I // 16], U16, name="offsets")
        nc.sync.dma_start(offsets[:], offs)

        key_word_pool = sb.tile([P, T], U16, name="key_word_pool")
        nc.sync.dma_start(key_word_pool[:].bitcast(I32), keys_words[0].bitcast(I32))
        query2_raw = load_rows("query2_raw", query2, "slot_a")
        query_raw = load_rows("query_raw", query, "slot_b")
        key_scale_pool = load_scale_rows("key_scale_pool", keys_scales, "slot_c")
        val_scale_pool = load_scale_rows("val_scale_pool", vals_scales, "slot_e")
        r = column("r")
        nc.gpsimd.dma_start(r[:], strict)

        query2_bf = round_rows("query2_bf", query2_raw, nc.scalar.copy, "slot_d")
        val_word_pool = sb.tile([P, T], U16, name="val_word_pool", tag="slot_a", align_bytes=64)
        nc.sync.dma_start(val_word_pool[:].bitcast(I32), vals_words[0].bitcast(I32))
        query_bf = round_rows("query_bf", query_raw, nc.scalar.copy, "query_bf")
        gout_raw = load_rows("gout_raw", gout, "slot_b")
        r_c, f_slope, f_offset = column("r_c"), column("f_slope"), column("f_offset")
        nc.gpsimd.tensor_scalar(r_c[:], r[:], CUBE_ROOT, 0.0, ALU.mult, ALU.add)
        nc.gpsimd.tensor_scalar(f_slope[:], r[:], -CUBE_ROOT, -CUBE_ROOT, ALU.mult, ALU.add)
        nc.gpsimd.tensor_scalar(f_offset[:], r[:], 0.0, CUBE_ROOT, ALU.mult, ALU.add)

        key_words = sb.tile([P, I], U16, name="key_words", align_bytes=64)
        nc.vector.tensor_copy(key_words[:], key_word_pool[:].indirect(offsets[:]))
        query2_mx = quantise("query2", query2_bf, "query2_codes")
        key_scales = sb.tile([P, I], U8, name="key_scales", tag="slot_d", align_bytes=64)
        b = [ps.tile([P, HALF], F32, name="b%d" % h) for h in range(2)]
        tanh_b, abs_tanh, neg_log = wide("tanh_b"), wide("abs_tanh"), wide("neg_log")
        for h, cols in enumerate(halves):
            nc.vector.tensor_copy(key_scales[:, cols],
                                  key_scale_pool[:].indirect(offsets[:, h * HALF // 16:(h + 1) * HALF // 16]))
            scores(b[h][:], query2_mx, key_words, key_scales, cols)
            nc.scalar.activation(tanh_b[:, cols], b[h][:], ACT.Tanh, scale=0.5)
            nc.scalar.activation(abs_tanh[:, cols], tanh_b[:, cols], ACT.Abs)
        for cols in halves:
            nc.scalar.activation(neg_log[:, cols], abs_tanh[:, cols], ACT.Ln, scale=0.5, bias=0.5)

        query_mx = quantise("query", query_bf, "slot_c")
        a = ps.tile([P, I], F32, name="a")
        scores(a[:], query_mx, key_words, key_scales, slice(0, I))

        base_sb = sb.tile([P, I], F32, name="base_sb", tag="slot_c", align_bytes=64)
        nc.sync.dma_start(base_sb[:], base)
        val_scales = sb.tile([P, I], U8, name="val_scales", align_bytes=64)
        nc.vector.tensor_copy(val_scales[:], val_scale_pool[:].indirect(offsets[:]))
        val_words = sb.tile([P, I], U16, name="val_words", tag="slot_e", align_bytes=64)
        nc.vector.tensor_copy(val_words[:], val_word_pool[:].indirect(offsets[:]))
        gout_bf = round_rows("gout_bf", gout_raw, nc.vector.tensor_copy, "slot_a")
        gout_mx = quantise("gout", gout_bf, "gout_codes")
        c0 = ps.tile([P, I], F32, name="c0")
        scores(c0[:], gout_mx, val_words, val_scales, slice(0, I))

        softplus = sb.tile([P, I], F32, name="softplus", tag="slot_b", align_bytes=64)
        neg_s, log_sig = wide("neg_s"), wide("log_sig")
        for h, cols in enumerate(halves):
            nc.vector.scalar_tensor_tensor(softplus[:, cols], b[h][:], 0.0, neg_log[:, cols], ALU.max, ALU.subtract)
        for cols in halves:
            nc.vector.scalar_tensor_tensor(neg_s[:, cols], softplus[:, cols], r[:], a[:, cols], ALU.mult, ALU.subtract)
        neg_max = column("neg_max")
        nc.vector.tensor_reduce(neg_max[:], neg_s[:], AX.X, ALU.min)
        p, z = wide("p"), column("z")
        nc.scalar.activation(p[:], neg_s[:], ACT.Exp, scale=-1.0, bias=neg_max[:], accum_out=z[:])
        for h, cols in enumerate(halves):
            nc.vector.scalar_tensor_tensor(log_sig[:, cols], b[h][:], 0.0, neg_log[:, cols], ALU.min, ALU.add)
        sig, f = wide("sig"), wide("f")
        nc.scalar.activation(sig[:], log_sig[:], ACT.Exp)
        nc.scalar.activation(f[:], sig[:], ACT.Identity, scale=f_slope[:], bias=f_offset[:])

        rz, pc_sum, c_mean, pc = column("rz"), column("pc_sum"), column("c_mean"), wide("pc")
        g, gu, w = wide("g"), wide("gu"), wide("w")
        nc.vector.scalar_tensor_tensor(pc[:], c0[:], 1.0, p[:], ALU.mult, ALU.mult, accum_out=pc_sum[:])
        nc.vector.reciprocal(rz[:], z[:])
        nc.vector.tensor_tensor(g[:, halves[0]], sig[:, halves[0]], p[:, halves[0]], ALU.mult)
        nc.vector.tensor_scalar(c_mean[:], pc_sum[:], rz[:], None, ALU.mult)
        nc.vector.tensor_tensor(g[:, halves[1]], sig[:, halves[1]], p[:, halves[1]], ALU.mult)
        rho, rho2, rho3 = column("rho"), column("rho2"), column("rho3")
        nc.scalar.activation(rho[:], rz[:], ACT.Copy, scale=r_c[:])
        nc.scalar.activation(rho2[:], rz[:], ACT.Square, scale=r_c[:])
        nc.scalar.activation(rho3[:], rho2[:], ACT.Copy, scale=rho[:])
        for cols in halves:
            nc.vector.scalar_tensor_tensor(gu[:, cols], c0[:, cols], c_mean[:], g[:, cols], ALU.subtract, ALU.mult)
        gu2, gu2_sum, b_sum = wide("gu2"), column("gu2_sum"), column("b_sum")
        nc.scalar.activation(gu2[:], gu[:], ACT.Square, scale=rho[:], accum_out=gu2_sum[:])
        nc.scalar.activation(b_sum[:], gu2_sum[:], ACT.Copy, scale=rho[:])
        ggu, a_sum = wide("ggu"), column("a_sum")

        def guf(cols):
            nc.vector.scalar_tensor_tensor(w[:, cols], gu[:, cols], rho2[:], f[:, cols], ALU.mult, ALU.mult)

        guf(halves[0])
        nc.vector.scalar_tensor_tensor(ggu[:], gu[:], rho3[:], g[:], ALU.mult, ALU.mult, accum_out=a_sum[:])
        guf(halves[1])
        part1, part2, res = wide("part1"), wide("part2"), wide("res")
        nc.vector.scalar_tensor_tensor(part1[:], g[:], b_sum[:], base_sb[:], ALU.mult, ALU.add)
        pieces = (slice(0, I - LAST), slice(I - LAST, I))
        for cols in pieces:
            nc.vector.scalar_tensor_tensor(part2[:, cols], w[:, cols], a_sum[:], gu[:, cols], ALU.add, ALU.mult)
        for cols, queue in zip(pieces, (nc.scalar, nc.sync)):
            nc.vector.tensor_tensor(res[:, cols], part1[:, cols], part2[:, cols], ALU.add)
            queue.dma_start(out[:, cols], res[:, cols])
